import numpy as np
import ml_dtypes


def mxq(x, axis, fmt="e4m3"):
    dtype, down = {"e4m3": (ml_dtypes.float8_e4m3fn, 7), "e5m2": (ml_dtypes.float8_e5m2, 14)}[fmt]
    v = np.moveaxis(np.asarray(x, np.float32).astype(ml_dtypes.bfloat16).astype(np.float64), axis, -1)
    blocks = v.reshape(v.shape[:-1] + (-1, 32))
    amax = np.abs(blocks).max(-1, keepdims=True)
    byte = np.maximum(np.where(amax > 0, np.frexp(amax)[1] - 1 + 127, 0) - down, 1)
    scale = np.exp2(byte - 127.0)
    codes = (blocks / scale).astype(np.float32).astype(dtype).astype(np.float64)
    return np.moveaxis((codes * scale).reshape(v.shape), -1, axis)


WIDE = False


def mx_kscale(k):
    if not WIDE:
        return np.ones(k)
    levels = np.array([10, -10, 5, -5, 0])
    if k % 512:
        return np.exp2(np.random.permutation(np.resize(levels, k // 32))).repeat(32)
    a = np.empty((k // 512, 16))
    for p in range(k // 512):
        a[p, :8] = np.random.permutation(np.resize(levels, 8))
        for g in range(8):
            far = levels[np.abs(levels - a[p, g]) >= 10]
            a[p, g + 8] = far[np.random.randint(len(far))]
    return np.exp2(a.ravel()).repeat(32)


def f64(x):
    return np.asarray(x).astype(np.float64)


def striped(idx):
    return np.tile(np.asarray(idx).reshape(-1, 16).T, (8, 1)).astype(np.uint16)


def unstriped(offs):
    return offs[:16].T.reshape(-1).astype(np.int64)


G, T, T2, D, M = 512, 1024, 2048, 1536, 128


def setup_inputs():
    n = np.random.standard_normal
    s = mx_kscale(D)[:, None]
    return {
        "xT": (n((D, T)) * s).astype(np.float32),
        "w": (n((D, M)) / np.sqrt(D) / s).astype(np.float32),
        "cache": n((M, T2)).astype(np.float32),
        "offs": striped(np.random.permutation(T)[:G]),
        "slots": striped(np.random.permutation(T2)[:G]),
    }


def reference(xT, w, cache, offs, slots):
    y = mxq(f64(w), 0, "e4m3").T @ mxq(f64(xT)[:, unstriped(offs)], 0, "e4m3")
    out = f64(cache).copy()
    out[:, unstriped(slots)] = y
    return out

@@ -1,0 +1,165 @@
+from contextlib import ExitStack
+
+import concourse.mybir as mybir
+
+D, T, M, G, T2 = 1536, 1024, 128, 512, 2048
+FLOPS = 2 * D * M * G
+
+F32 = mybir.dt.float32
+BF16 = mybir.dt.bfloat16
+U32 = mybir.dt.uint32
+U16 = mybir.dt.uint16
+U8 = mybir.dt.uint8
+FP8X4 = mybir.dt.float8_e4m3fn_x4
+COPY = mybir.ActivationFunctionType.Copy
+
+P = 128
+PACK = 4
+PASSES = D // (P * PACK)
+HALF = G // 2
+
+
+def tile_attend_fill_kernel(tc, xT, w, cache, offs, slots, out):
+    nc = tc.nc
+    x_rows = xT.rearrange("(g p j) c -> g p j c", p=P, j=PACK)
+    w_rows = w.rearrange("(g p j) m -> p g (j m)", p=P, j=PACK)
+
+    with ExitStack() as ctx:
+        keep = ctx.enter_context(tc.tile_pool(name="keep", bufs=1))
+        psum = ctx.enter_context(tc.psum_pool(name="psum", bufs=1))
+
+        offs_t = keep.tile([P, G // 16], U16, name="offs_t")
+        slots_t = keep.tile([P, G // 16], U16, name="slots_t")
+        w_raw = keep.tile([P, PASSES, PACK * M], F32, name="w_raw")
+        w_grouped = keep.tile([P, PASSES, M, PACK], BF16, name="w_grouped", align_bytes=64)
+        w_codes = keep.tile([P, PASSES * M], U32, name="w_codes", align_bytes=64)
+        w_scales = keep.tile([P, PASSES * M], U8, name="w_scales", align_bytes=64)
+        window = keep.tile([P, T2], F32, name="window")
+        y = [keep.tile([P, HALF], F32, name=f"y{h}") for h in range(2)]
+        acc = [psum.tile([M, HALF], F32, name=f"acc{h}") for h in range(2)]
+        raw, pairs = {}, {}
+        grouped, codes, scales = {}, {}, {}
+        for u in [1,2,3,4,5]:
+            raw[u] = keep.tile([P, 2, T], F32, name=f"raw{u}")
+            pairs[u] = keep.tile([P, 2 * T], BF16, name=f"pairs{u}", align_bytes=64)
+        for u in [0]:
+            for j in range(2):
+                raw[u, j] = keep.tile([P, T], F32, name=f"raw{u}_{j}")
+        for g in range(PASSES):
+            for h in range(2 if g == 1 else 1):
+                n = HALF if g == 1 else G
+                grouped[g, h] = keep.tile([P, n, PACK], BF16, name=f"grouped{g}_{h}", align_bytes=64)
+                codes[g, h] = keep.tile([P, n], U32, name=f"codes{g}_{h}", align_bytes=64)
+                scales[g, h] = keep.tile([P, n], U8, name=f"scales{g}_{h}", align_bytes=64)
+
+        def load_pair(u):
+            nc.sync.dma_start(out=raw[u][:], in_=x_rows[u // 2, :, 2 * (u % 2) : 2 * (u % 2) + 2, :])
+
+        def load_plane(u, j):
+            nc.sync.dma_start(out=raw[u, j][:], in_=x_rows[u // 2, :, 2 * (u % 2) + j, :])
+
+        def load_w(g0, g1):
+            nc.sync.dma_start(out=w_raw[:, g0:g1, :], in_=w_rows[:, g0:g1, :])
+
+        def cast_s(u, cut):
+            src = raw[u][:].rearrange("p t c -> p c t")
+            dst = pairs[u][:].rearrange("p (c t) -> p c t", t=2)
+            nc.scalar.activation(dst[:, 0:cut, :], src[:, 0:cut, :], COPY)
+
+        def cast_v(u, cut):
+            src = raw[u][:].rearrange("p t c -> p c t")
+            dst = pairs[u][:].rearrange("p (c t) -> p c t", t=2)
+            nc.vector.tensor_copy(out=dst[:, cut:T, :], in_=src[:, cut:T, :])
+
+        def gather_pair(u, h, n):
+            words = grouped[u // 2, h][:].rearrange("p n t -> p (n t)").bitcast(U32).rearrange("p (n h) -> p n h", h=2)
+            nc.vector.tensor_copy(
+                words[:, :, u % 2], pairs[u][:].bitcast(U32).indirect(offs_t[:, h * n // 16 : (h + 1) * n // 16])
+            )
+
+        def gather_plane(u, j, h, n):
+            nc.vector.tensor_copy(
+                grouped[u // 2, h][:, :, 2 * (u % 2) + j],
+                raw[u, j][:].indirect(offs_t[:, h * n // 16 : (h + 1) * n // 16]),
+            )
+
+        def quantize(g, h):
+            nc.vector.quantize_mx(
+                out=codes[g, h][:].bitcast(FP8X4),
+                scales=scales[g, h][:],
+                in_=grouped[g, h][:].rearrange("p n t -> p (n t)"),
+            )
+
+        def cast_w(engine_copy, g0, g1):
+            engine_copy(w_grouped[:, g0:g1, :, :], w_raw[:, g0:g1, :].rearrange("p g (j m) -> p g m j", j=PACK))
+
+        def quantize_w(g0, g1):
+            cols = slice(g0 * M, g1 * M)
+            nc.vector.quantize_mx(
+                out=w_codes[:, cols].bitcast(FP8X4),
+                scales=w_scales[:, cols],
+                in_=w_grouped[:, g0:g1, :, :].rearrange("p g m j -> p (g m j)"),
+            )
+
+        def multiply(g, h, start, stop):
+            split = g == 1
+            cols = slice(0, HALF) if split else slice(h * HALF, (h + 1) * HALF)
+            nc.tensor.matmul_mx(
+                out=acc[h][:],
+                lhsT=w_codes[:, g * M : (g + 1) * M].bitcast(FP8X4),
+                lhsT_scale=w_scales[:, g * M : (g + 1) * M],
+                rhs=codes[g, h if split else 0][:, cols].bitcast(FP8X4),
+                rhs_scale=scales[g, h if split else 0][:, cols],
+                start=start,
+                stop=stop,
+            )
+
+        nc.sync.dma_start(offs_t[:], offs)
+        load_plane(0, 1)
+        load_plane(0, 0)
+        load_pair(1)
+        load_pair(5)
+        load_w(0, 2)
+        load_pair(4)
+        load_pair(3)
+        load_pair(2)
+        load_w(2, 3)
+        nc.sync.dma_start(slots_t[:], slots)
+        nc.sync.dma_start(out=window[:], in_=cache)
+        gather_plane(0, 1, 0, G)
+        gather_plane(0, 0, 0, G)
+        cast_s(1, 512)
+        cast_v(1, 512)
+        gather_pair(1, 0, G)
+        cast_s(5, 640)
+        cast_v(5, 640)
+        quantize(0, 0)
+        cast_w(nc.scalar.copy, 0, 2)
+        gather_pair(5, 0, G)
+        cast_s(4, 512)
+        cast_v(4, 512)
+        quantize_w(0, 2)
+        for h in range(2):
+            multiply(0, h, True, False)
+        gather_pair(4, 0, G)
+        cast_s(3, 768)
+        cast_v(3, 768)
+        quantize(2, 0)
+        gather_pair(3, 0, HALF)
+        gather_pair(3, 1, HALF)
+        cast_s(2, 768)
+        cast_w(nc.vector.tensor_copy, 2, 3)
+        cast_v(2, 768)
+        quantize_w(2, 3)
+        for h in range(2):
+            multiply(2, h, False, False)
+        gather_pair(2, 0, HALF)
+        quantize(1, 0)
+        gather_pair(2, 1, HALF)
+        quantize(1, 1)
+        for h in range(2):
+            multiply(1, h, False, True)
+            nc.scalar.copy(y[h][:], acc[h][:])
+            nc.vector.tensor_copy(window[:].indirect(slots_t[:, 16 * h : 16 * h + 16]), y[h][:])
+        nc.sync.dma_start(out=out[:, 0 : T2 // 2], in_=window[:, 0 : T2 // 2])
+        nc.scalar.dma_start(out=out[:, T2 // 2 : T2], in_=window[:, T2 // 2 : T2])

@@ -38,17 +38,20 @@ def tile_attend_fill_kernel(tc, xT, w, cache, offs, slots, out):
         y = [keep.tile([P, HALF], F32, name=f"y{h}") for h in range(2)]
         acc = [psum.tile([M, HALF], F32, name=f"acc{h}") for h in range(2)]
         raw, pairs = {}, {}
-        grouped, codes, scales = {}, {}, {}
-        for u in [1,2,3,4,5]:
+        grouped, codes, scales, parts = {}, {}, {}, {}
+        merged = [1]
+        for u in [0,1,4,5]:
             raw[u] = keep.tile([P, 2, T], F32, name=f"raw{u}")
             pairs[u] = keep.tile([P, 2 * T], BF16, name=f"pairs{u}", align_bytes=64)
-        for u in [0]:
+        for u in [2,3]:
             for j in range(2):
                 raw[u, j] = keep.tile([P, T], F32, name=f"raw{u}_{j}")
         for g in range(PASSES):
-            for h in range(2 if g == 1 else 1):
-                n = HALF if g == 1 else G
+            for h in range(2 if g == 0 else 1):
+                n = HALF if g == 0 else G
                 grouped[g, h] = keep.tile([P, n, PACK], BF16, name=f"grouped{g}_{h}", align_bytes=64)
+                if g in merged:
+                    parts[g, h] = keep.tile([P, 2, n, 2], BF16, name=f"parts{g}_{h}", align_bytes=64)
                 codes[g, h] = keep.tile([P, n], U32, name=f"codes{g}_{h}", align_bytes=64)
                 scales[g, h] = keep.tile([P, n], U8, name=f"scales{g}_{h}", align_bytes=64)
 
@@ -72,15 +75,27 @@ def tile_attend_fill_kernel(tc, xT, w, cache, offs, slots, out):
             nc.vector.tensor_copy(out=dst[:, cut:T, :], in_=src[:, cut:T, :])
 
         def gather_pair(u, h, n):
-            words = grouped[u // 2, h][:].rearrange("p n t -> p (n t)").bitcast(U32).rearrange("p (n h) -> p n h", h=2)
-            nc.vector.tensor_copy(
-                words[:, :, u % 2], pairs[u][:].bitcast(U32).indirect(offs_t[:, h * n // 16 : (h + 1) * n // 16])
-            )
+            g = u // 2
+            if g in merged:
+                words = parts[g, h][:, u % 2, :, :].rearrange("p n t -> p (n t)").bitcast(U32)
+            else:
+                words = grouped[g, h][:].rearrange("p n t -> p (n t)").bitcast(U32).rearrange("p (n h) -> p n h", h=2)[:, :, u % 2]
+            nc.vector.tensor_copy(words, pairs[u][:].bitcast(U32).indirect(offs_t[:, h * n // 16 : (h + 1) * n // 16]))
 
         def gather_plane(u, j, h, n):
+            g = u // 2
+            dst = parts[g, h][:, u % 2, :, j] if g in merged else grouped[g, h][:, :, 2 * (u % 2) + j]
+            nc.vector.tensor_copy(dst, raw[u, j][:].indirect(offs_t[:, h * n // 16 : (h + 1) * n // 16]))
+
+        def merge_v(g, h):
             nc.vector.tensor_copy(
-                grouped[u // 2, h][:, :, 2 * (u % 2) + j],
-                raw[u, j][:].indirect(offs_t[:, h * n // 16 : (h + 1) * n // 16]),
+                out=grouped[g, h][:].rearrange("p n t -> p (n t)").bitcast(F32).rearrange("p (n h) -> p n h", h=2),
+                in_=parts[g, h][:].rearrange("p h n t -> p (h n t)").bitcast(F32).rearrange("p (h n) -> p n h", h=2),
+            )
+
+        def merge_s(g, h):
+            nc.scalar.copy(
+                grouped[g, h][:].rearrange("p n (h t) -> p n h t", h=2), parts[g, h][:].rearrange("p h n t -> p n h t")
             )
 
         def quantize(g, h):
@@ -102,7 +117,7 @@ def tile_attend_fill_kernel(tc, xT, w, cache, offs, slots, out):
             )
 
         def multiply(g, h, start, stop):
-            split = g == 1
+            split = g == 0
             cols = slice(0, HALF) if split else slice(h * HALF, (h + 1) * HALF)
             nc.tensor.matmul_mx(
                 out=acc[h][:],
@@ -115,50 +130,49 @@ def tile_attend_fill_kernel(tc, xT, w, cache, offs, slots, out):
             )
 
         nc.sync.dma_start(offs_t[:], offs)
-        load_plane(0, 1)
-        load_plane(0, 0)
-        load_pair(1)
+        load_plane(2, 1)
+        load_plane(3, 0)
+        load_plane(2, 0)
+        load_plane(3, 1)
         load_pair(5)
-        load_w(0, 2)
+        load_pair(0)
         load_pair(4)
-        load_pair(3)
-        load_pair(2)
+        load_w(0, 2)
+        load_pair(1)
         load_w(2, 3)
         nc.sync.dma_start(slots_t[:], slots)
         nc.sync.dma_start(out=window[:], in_=cache)
-        gather_plane(0, 1, 0, G)
-        gather_plane(0, 0, 0, G)
-        cast_s(1, 512)
-        cast_v(1, 512)
-        gather_pair(1, 0, G)
-        cast_s(5, 640)
-        cast_v(5, 640)
-        quantize(0, 0)
-        cast_w(nc.scalar.copy, 0, 2)
+        gather_plane(3, 0, 0, G)
+        gather_plane(2, 1, 0, G)
+        gather_plane(2, 0, 0, G)
+        gather_plane(3, 1, 0, G)
+        merge_v(1, 0)
+        quantize(1, 0)
+        cast_s(5, 768)
+        cast_v(5, 768)
         gather_pair(5, 0, G)
-        cast_s(4, 512)
-        cast_v(4, 512)
+        cast_s(0, 1024)
+        cast_s(4, 640)
+        cast_v(4, 640)
+        gather_pair(0, 1, HALF)
+        gather_pair(0, 0, HALF)
+        gather_pair(4, 0, G)
+        cast_w(nc.scalar.copy, 0, 2)
+        cast_w(nc.vector.tensor_copy, 2, 3)
+        quantize_w(2, 3)
+        quantize(2, 0)
         quantize_w(0, 2)
         for h in range(2):
-            multiply(0, h, True, False)
-        gather_pair(4, 0, G)
-        cast_s(3, 768)
-        cast_v(3, 768)
-        quantize(2, 0)
-        gather_pair(3, 0, HALF)
-        gather_pair(3, 1, HALF)
-        cast_s(2, 768)
-        cast_w(nc.vector.tensor_copy, 2, 3)
-        cast_v(2, 768)
-        quantize_w(2, 3)
+            multiply(1, h, True, False)
         for h in range(2):
             multiply(2, h, False, False)
-        gather_pair(2, 0, HALF)
-        quantize(1, 0)
-        gather_pair(2, 1, HALF)
-        quantize(1, 1)
+        cast_s(1, 1024)
+        gather_pair(1, 0, HALF)
+        quantize(0, 0)
+        gather_pair(1, 1, HALF)
+        quantize(0, 1)
         for h in range(2):
-            multiply(1, h, False, True)
+            multiply(0, h, False, True)
             nc.scalar.copy(y[h][:], acc[h][:])
             nc.vector.tensor_copy(window[:].indirect(slots_t[:, 16 * h : 16 * h + 16]), y[h][:])
         nc.sync.dma_start(out=out[:, 0 : T2 // 2], in_=window[:, 0 : T2 // 2])

@@ -40,15 +40,19 @@ def tile_attend_fill_kernel(tc, xT, w, cache, offs, slots, out):
         raw, pairs = {}, {}
         grouped, codes, scales, parts = {}, {}, {}, {}
         merged = [1]
-        for u in [0,1,4,5]:
+        for u in []:
             raw[u] = keep.tile([P, 2, T], F32, name=f"raw{u}")
             pairs[u] = keep.tile([P, 2 * T], BF16, name=f"pairs{u}", align_bytes=64)
-        for u in [2,3]:
+        for u in [0,1,2,3,4,5]:
             for j in range(2):
                 raw[u, j] = keep.tile([P, T], F32, name=f"raw{u}_{j}")
+        planes = {}
+        for u in [0,4]:
+            for j in range(2):
+                planes[u, j] = keep.tile([P, T], BF16, name=f"plane{u}_{j}", align_bytes=64)
         for g in range(PASSES):
-            for h in range(2 if g == 0 else 1):
-                n = HALF if g == 0 else G
+            for h in range(2 if g == 2 else 1):
+                n = HALF if g == 2 else G
                 grouped[g, h] = keep.tile([P, n, PACK], BF16, name=f"grouped{g}_{h}", align_bytes=64)
                 if g in merged:
                     parts[g, h] = keep.tile([P, 2, n, 2], BF16, name=f"parts{g}_{h}", align_bytes=64)
@@ -117,7 +121,7 @@ def tile_attend_fill_kernel(tc, xT, w, cache, offs, slots, out):
             )
 
         def multiply(g, h, start, stop):
-            split = g == 0
+            split = g == 2
             cols = slice(0, HALF) if split else slice(h * HALF, (h + 1) * HALF)
             nc.tensor.matmul_mx(
                 out=acc[h][:],
@@ -129,50 +133,77 @@ def tile_attend_fill_kernel(tc, xT, w, cache, offs, slots, out):
                 stop=stop,
             )
 
+        def cast_plane_s(u, j, cut):
+            nc.scalar.activation(planes[u, j][:, 0:cut], raw[u, j][:, 0:cut], COPY)
+
+        def cast_plane_v(u, j, cut):
+            nc.vector.tensor_copy(out=planes[u, j][:, cut:T], in_=raw[u, j][:, cut:T])
+
+        def gather_s(u, j, h, n):
+            g = u // 2
+            dst = parts[g, h][:, u % 2, :, j] if g in merged else grouped[g, h][:, :, 2 * (u % 2) + j]
+            nc.scalar.activation(dst, planes[u, j][:].indirect(offs_t[:, h * n // 16 : (h + 1) * n // 16]), COPY)
+
+        def merge_g(g, h):
+            nc.gpsimd.tensor_copy(
+                out=grouped[g, h][:].rearrange("p n t -> p (n t)").bitcast(U32).rearrange("p (n h) -> p n h", h=2),
+                in_=parts[g, h][:].rearrange("p h n t -> p (h n t)").bitcast(U32).rearrange("p (h n) -> p n h", h=2),
+            )
+
         nc.sync.dma_start(offs_t[:], offs)
-        load_plane(2, 1)
-        load_plane(3, 0)
+        load_plane(1, 1)
+        load_plane(0, 0)
+        load_plane(5, 0)
+        load_plane(4, 0)
         load_plane(2, 0)
         load_plane(3, 1)
-        load_pair(5)
-        load_pair(0)
-        load_pair(4)
-        load_w(0, 2)
-        load_pair(1)
+        load_plane(2, 1)
+        load_plane(3, 0)
+        load_plane(0, 1)
+        load_plane(1, 0)
+        load_w(1, 2)
+        load_w(0, 1)
+        load_plane(4, 1)
         load_w(2, 3)
+        load_plane(5, 1)
         nc.sync.dma_start(slots_t[:], slots)
         nc.sync.dma_start(out=window[:], in_=cache)
-        gather_plane(3, 0, 0, G)
-        gather_plane(2, 1, 0, G)
+        gather_plane(1, 1, 0, G)
+        cast_plane_s(0, 0, 1024)
+        gather_plane(5, 0, 1, HALF)
+        gather_plane(5, 0, 0, HALF)
+        cast_plane_s(4, 0, 1024)
         gather_plane(2, 0, 0, G)
+        gather_s(4, 0, 0, HALF)
         gather_plane(3, 1, 0, G)
+        gather_s(0, 0, 0, G)
+        gather_plane(2, 1, 0, G)
+        gather_s(4, 0, 1, HALF)
+        gather_plane(3, 0, 0, G)
+        cast_plane_s(0, 1, 1024)
         merge_v(1, 0)
+        gather_s(0, 1, 0, G)
+        gather_plane(1, 0, 0, G)
+        cast_w(nc.gpsimd.tensor_copy, 1, 2)
+        cast_w(nc.gpsimd.tensor_copy, 0, 1)
         quantize(1, 0)
-        cast_s(5, 768)
-        cast_v(5, 768)
-        gather_pair(5, 0, G)
-        cast_s(0, 1024)
-        cast_s(4, 640)
-        cast_v(4, 640)
-        gather_pair(0, 1, HALF)
-        gather_pair(0, 0, HALF)
-        gather_pair(4, 0, G)
-        cast_w(nc.scalar.copy, 0, 2)
-        cast_w(nc.vector.tensor_copy, 2, 3)
-        quantize_w(2, 3)
-        quantize(2, 0)
+        cast_plane_s(4, 1, 1024)
+        quantize(0, 0)
+        cast_w(nc.gpsimd.tensor_copy, 2, 3)
+        gather_s(4, 1, 0, HALF)
+        gather_plane(5, 1, 0, HALF)
         quantize_w(0, 2)
         for h in range(2):
             multiply(1, h, True, False)
         for h in range(2):
-            multiply(2, h, False, False)
-        cast_s(1, 1024)
-        gather_pair(1, 0, HALF)
-        quantize(0, 0)
-        gather_pair(1, 1, HALF)
-        quantize(0, 1)
+            multiply(0, h, False, False)
+        quantize_w(2, 3)
+        gather_s(4, 1, 1, HALF)
+        quantize(2, 0)
+        gather_plane(5, 1, 1, HALF)
+        quantize(2, 1)
         for h in range(2):
-            multiply(0, h, False, True)
+            multiply(2, h, False, True)
             nc.scalar.copy(y[h][:], acc[h][:])
             nc.vector.tensor_copy(window[:].indirect(slots_t[:, 16 * h : 16 * h + 16]), y[h][:])
         nc.sync.dma_start(out=out[:, 0 : T2 // 2], in_=window[:, 0 : T2 // 2])

@@ -109,6 +109,9 @@ def tile_attend_fill_kernel(tc, xT, w, cache, offs, slots, out):
                 in_=grouped[g, h][:].rearrange("p n t -> p (n t)"),
             )
 
+        def round_gpsimd(dst, src):
+            nc.gpsimd.tensor_scalar(dst, src, 1.0, 0.0, mybir.AluOpType.mult, mybir.AluOpType.add)
+
         def cast_w(engine_copy, g0, g1):
             engine_copy(w_grouped[:, g0:g1, :, :], w_raw[:, g0:g1, :].rearrange("p g (j m) -> p g m j", j=PACK))
 
@@ -184,12 +187,12 @@ def tile_attend_fill_kernel(tc, xT, w, cache, offs, slots, out):
         merge_v(1, 0)
         gather_s(0, 1, 0, G)
         gather_plane(1, 0, 0, G)
-        cast_w(nc.gpsimd.tensor_copy, 1, 2)
-        cast_w(nc.gpsimd.tensor_copy, 0, 1)
+        cast_w(round_gpsimd, 1, 2)
+        cast_w(round_gpsimd, 0, 1)
         quantize(1, 0)
         cast_plane_s(4, 1, 1024)
         quantize(0, 0)
-        cast_w(nc.gpsimd.tensor_copy, 2, 3)
+        cast_w(round_gpsimd, 2, 3)
         gather_s(4, 1, 0, HALF)
         gather_plane(5, 1, 0, HALF)
         quantize_w(0, 2)

from contextlib import ExitStack

import concourse.mybir as mybir

D, T, M, G, T2 = 1536, 1024, 128, 512, 2048
FLOPS = 2 * D * M * G

F32 = mybir.dt.float32
BF16 = mybir.dt.bfloat16
U32 = mybir.dt.uint32
U16 = mybir.dt.uint16
U8 = mybir.dt.uint8
FP8X4 = mybir.dt.float8_e4m3fn_x4
COPY = mybir.ActivationFunctionType.Copy

P = 128
PACK = 4
PASSES = D // (P * PACK)
HALF = G // 2


def tile_attend_fill_kernel(tc, xT, w, cache, offs, slots, out):
    nc = tc.nc
    x_rows = xT.rearrange("(g p j) c -> g p j c", p=P, j=PACK)
    w_rows = w.rearrange("(g p j) m -> p g (j m)", p=P, j=PACK)

    with ExitStack() as ctx:
        keep = ctx.enter_context(tc.tile_pool(name="keep", bufs=1))
        psum = ctx.enter_context(tc.psum_pool(name="psum", bufs=1))

        offs_t = keep.tile([P, G // 16], U16, name="offs_t")
        slots_t = keep.tile([P, G // 16], U16, name="slots_t")
        w_raw = keep.tile([P, PASSES, PACK * M], F32, name="w_raw")
        w_grouped = keep.tile([P, PASSES, M, PACK], BF16, name="w_grouped", align_bytes=64)
        w_codes = keep.tile([P, PASSES * M], U32, name="w_codes", align_bytes=64)
        w_scales = keep.tile([P, PASSES * M], U8, name="w_scales", align_bytes=64)
        window = keep.tile([P, T2], F32, name="window")
        y = [keep.tile([P, HALF], F32, name=f"y{h}") for h in range(2)]
        acc = [psum.tile([M, HALF], F32, name=f"acc{h}") for h in range(2)]
        raw, pairs = {}, {}
        grouped, codes, scales, parts = {}, {}, {}, {}
        merged = [1]
        for u in []:
            raw[u] = keep.tile([P, 2, T], F32, name=f"raw{u}")
            pairs[u] = keep.tile([P, 2 * T], BF16, name=f"pairs{u}", align_bytes=64)
        for u in [0,1,2,3,4,5]:
            for j in range(2):
                raw[u, j] = keep.tile([P, T], F32, name=f"raw{u}_{j}")
        planes = {}
        for u in [0,4]:
            for j in range(2):
                planes[u, j] = keep.tile([P, T], BF16, name=f"plane{u}_{j}", align_bytes=64)
        for g in range(PASSES):
            for h in range(2 if g == 2 else 1):
                n = HALF if g == 2 else G
                grouped[g, h] = keep.tile([P, n, PACK], BF16, name=f"grouped{g}_{h}", align_bytes=64)
                if g in merged:
                    parts[g, h] = keep.tile([P, 2, n, 2], BF16, name=f"parts{g}_{h}", align_bytes=64)
                codes[g, h] = keep.tile([P, n], U32, name=f"codes{g}_{h}", align_bytes=64)
                scales[g, h] = keep.tile([P, n], U8, name=f"scales{g}_{h}", align_bytes=64)

        def load_pair(u):
            nc.sync.dma_start(out=raw[u][:], in_=x_rows[u // 2, :, 2 * (u % 2) : 2 * (u % 2) + 2, :])

        def load_plane(u, j):
            nc.sync.dma_start(out=raw[u, j][:], in_=x_rows[u // 2, :, 2 * (u % 2) + j, :])

        def load_w(g0, g1):
            nc.sync.dma_start(out=w_raw[:, g0:g1, :], in_=w_rows[:, g0:g1, :])

        def cast_s(u, cut):
            src = raw[u][:].rearrange("p t c -> p c t")
            dst = pairs[u][:].rearrange("p (c t) -> p c t", t=2)
            nc.scalar.activation(dst[:, 0:cut, :], src[:, 0:cut, :], COPY)

        def cast_v(u, cut):
            src = raw[u][:].rearrange("p t c -> p c t")
            dst = pairs[u][:].rearrange("p (c t) -> p c t", t=2)
            nc.vector.tensor_copy(out=dst[:, cut:T, :], in_=src[:, cut:T, :])

        def gather_pair(u, h, n):
            g = u // 2
            if g in merged:
                words = parts[g, h][:, u % 2, :, :].rearrange("p n t -> p (n t)").bitcast(U32)
            else:
                words = grouped[g, h][:].rearrange("p n t -> p (n t)").bitcast(U32).rearrange("p (n h) -> p n h", h=2)[:, :, u % 2]
            nc.vector.tensor_copy(words, pairs[u][:].bitcast(U32).indirect(offs_t[:, h * n // 16 : (h + 1) * n // 16]))

        def gather_plane(u, j, h, n):
            g = u // 2
            dst = parts[g, h][:, u % 2, :, j] if g in merged else grouped[g, h][:, :, 2 * (u % 2) + j]
            nc.vector.tensor_copy(dst, raw[u, j][:].indirect(offs_t[:, h * n // 16 : (h + 1) * n // 16]))

        def merge_v(g, h):
            nc.vector.tensor_copy(
                out=grouped[g, h][:].rearrange("p n t -> p (n t)").bitcast(F32).rearrange("p (n h) -> p n h", h=2),
                in_=parts[g, h][:].rearrange("p h n t -> p (h n t)").bitcast(F32).rearrange("p (h n) -> p n h", h=2),
            )

        def merge_s(g, h):
            nc.scalar.copy(
                grouped[g, h][:].rearrange("p n (h t) -> p n h t", h=2), parts[g, h][:].rearrange("p h n t -> p n h t")
            )

        def quantize(g, h):
            nc.vector.quantize_mx(
                out=codes[g, h][:].bitcast(FP8X4),
                scales=scales[g, h][:],
                in_=grouped[g, h][:].rearrange("p n t -> p (n t)"),
            )

        def round_gpsimd(dst, src):
            nc.gpsimd.tensor_scalar(dst, src, 1.0, 0.0, mybir.AluOpType.mult, mybir.AluOpType.add)

        def cast_w(engine_copy, g0, g1):
            engine_copy(w_grouped[:, g0:g1, :, :], w_raw[:, g0:g1, :].rearrange("p g (j m) -> p g m j", j=PACK))

        def quantize_w(g0, g1):
            cols = slice(g0 * M, g1 * M)
            nc.vector.quantize_mx(
                out=w_codes[:, cols].bitcast(FP8X4),
                scales=w_scales[:, cols],
                in_=w_grouped[:, g0:g1, :, :].rearrange("p g m j -> p (g m j)"),
            )

        def multiply(g, h, start, stop):
            split = g == 2
            cols = slice(0, HALF) if split else slice(h * HALF, (h + 1) * HALF)
            nc.tensor.matmul_mx(
                out=acc[h][:],
                lhsT=w_codes[:, g * M : (g + 1) * M].bitcast(FP8X4),
                lhsT_scale=w_scales[:, g * M : (g + 1) * M],
                rhs=codes[g, h if split else 0][:, cols].bitcast(FP8X4),
                rhs_scale=scales[g, h if split else 0][:, cols],
                start=start,
                stop=stop,
            )

        def cast_plane_s(u, j, cut):
            nc.scalar.activation(planes[u, j][:, 0:cut], raw[u, j][:, 0:cut], COPY)

        def cast_plane_v(u, j, cut):
            nc.vector.tensor_copy(out=planes[u, j][:, cut:T], in_=raw[u, j][:, cut:T])

        def gather_s(u, j, h, n):
            g = u // 2
            dst = parts[g, h][:, u % 2, :, j] if g in merged else grouped[g, h][:, :, 2 * (u % 2) + j]
            nc.scalar.activation(dst, planes[u, j][:].indirect(offs_t[:, h * n // 16 : (h + 1) * n // 16]), COPY)

        def merge_g(g, h):
            nc.gpsimd.tensor_copy(
                out=grouped[g, h][:].rearrange("p n t -> p (n t)").bitcast(U32).rearrange("p (n h) -> p n h", h=2),
                in_=parts[g, h][:].rearrange("p h n t -> p (h n t)").bitcast(U32).rearrange("p (h n) -> p n h", h=2),
            )

        nc.sync.dma_start(offs_t[:], offs)
        load_plane(1, 1)
        load_plane(0, 0)
        load_plane(5, 0)
        load_plane(4, 0)
        load_plane(2, 0)
        load_plane(3, 1)
        load_plane(2, 1)
        load_plane(3, 0)
        load_plane(0, 1)
        load_plane(1, 0)
        load_w(1, 2)
        load_w(0, 1)
        load_plane(4, 1)
        load_w(2, 3)
        load_plane(5, 1)
        nc.sync.dma_start(slots_t[:], slots)
        nc.sync.dma_start(out=window[:], in_=cache)
        gather_plane(1, 1, 0, G)
        cast_plane_s(0, 0, 1024)
        gather_plane(5, 0, 1, HALF)
        gather_plane(5, 0, 0, HALF)
        cast_plane_s(4, 0, 1024)
        gather_plane(2, 0, 0, G)
        gather_s(4, 0, 0, HALF)
        gather_plane(3, 1, 0, G)
        gather_s(0, 0, 0, G)
        gather_plane(2, 1, 0, G)
        gather_s(4, 0, 1, HALF)
        gather_plane(3, 0, 0, G)
        cast_plane_s(0, 1, 1024)
        merge_v(1, 0)
        gather_s(0, 1, 0, G)
        gather_plane(1, 0, 0, G)
        cast_w(round_gpsimd, 1, 2)
        cast_w(round_gpsimd, 0, 1)
        quantize(1, 0)
        cast_plane_s(4, 1, 1024)
        quantize(0, 0)
        cast_w(round_gpsimd, 2, 3)
        gather_s(4, 1, 0, HALF)
        gather_plane(5, 1, 0, HALF)
        quantize_w(0, 2)
        for h in range(2):
            multiply(1, h, True, False)
        for h in range(2):
            multiply(0, h, False, False)
        quantize_w(2, 3)
        gather_s(4, 1, 1, HALF)
        quantize(2, 0)
        gather_plane(5, 1, 1, HALF)
        quantize(2, 1)
        for h in range(2):
            multiply(2, h, False, True)
            nc.scalar.copy(y[h][:], acc[h][:])
            nc.vector.tensor_copy(window[:].indirect(slots_t[:, 16 * h : 16 * h + 16]), y[h][:])
        nc.sync.dma_start(out=out[:, 0 : T2 // 2], in_=window[:, 0 : T2 // 2])
        nc.scalar.dma_start(out=out[:, T2 // 2 : T2], in_=window[:, T2 // 2 : T2])
